import numpy as np
import ml_dtypes

BF16 = ml_dtypes.bfloat16


def bf(x):
    return np.asarray(x, np.float32).astype(BF16)


def f32(x):
    return np.asarray(x, np.float32)


def f64(x):
    return np.asarray(x).astype(np.float64)


def striped(idx):
    return np.concatenate([l.reshape(-1, 16).T for l in idx])


def rows(idx, k):
    return np.tile(np.repeat(idx, 16, axis=0), (k // (16 * 8), 1))


def look(tab, idx):
    return np.take_along_axis(f64(tab), rows(idx, len(tab)), axis=1)


K, S, V, N = 256, 2048, 2048, 2048


def setup_inputs():
    return {"tab": f32(np.random.standard_normal((2, K, S))), "offs": striped(np.stack([np.random.permutation(S)[:N] for _ in range(8)]))}


def reference(tab, offs):
    idx = np.stack([g.T.reshape(-1) for g in np.split(offs, 8)])
    x = (np.minimum(np.maximum(look(tab[0], idx), -1.25), 1.0)) * (np.maximum(look(tab[1], idx), 0.0))
    return x

@@ -1,0 +1,55 @@
+import concourse.mybir as mybir
+
+F32 = mybir.dt.float32
+U16 = mybir.dt.uint16
+MAX = mybir.AluOpType.max
+MIN = mybir.AluOpType.min
+MULT = mybir.AluOpType.mult
+RELU = mybir.ActivationFunctionType.Relu
+
+P = 128
+PIECE = 512
+STRIPE = 16
+
+FLOPS = 4 * 256 * 2048
+
+
+def tile_lookup_vg_cliprelu_out_kernel(tc, tab, offs, out):
+    nc = tc.nc
+    rows, places = tab.shape[1], tab.shape[2]
+    n = out.shape[1]
+    blocks = rows // P
+    pieces = n // PIECE
+    columns = PIECE // STRIPE
+
+    with (
+        tc.tile_pool(name="held", bufs=1) as held,
+        tc.tile_pool(name="work", bufs=blocks * pieces) as work,
+    ):
+        offsets = held.tile([P, n // STRIPE], U16, name="offsets")
+        nc.sync.dma_start(offsets[:], offs)
+
+        values = []
+        gates = []
+        for b in range(blocks):
+            value = held.tile([P, places], F32, name=f"value{b}")
+            nc.sync.dma_start(value[:], tab[0, b * P : (b + 1) * P, :])
+            values.append(value)
+            gate = held.tile([P, places], F32, name=f"gate{b}")
+            nc.sync.dma_start(gate[:], tab[1, b * P : (b + 1) * P, :])
+            gates.append(gate)
+
+        for b in range(blocks):
+            for k in range(pieces):
+                piece = offsets[:, k * columns : (k + 1) * columns]
+                clamped = work.tile([P, PIECE], F32, name="clamped")
+                nc.vector.tensor_scalar(
+                    clamped[:], values[b][:].indirect(piece), -1.25, 1.0, MAX, MIN
+                )
+                opened = work.tile([P, PIECE], F32, name="opened")
+                nc.scalar.activation(opened[:], gates[b][:].indirect(piece), RELU)
+                product = work.tile([P, PIECE], F32, name="product")
+                nc.vector.tensor_tensor(product[:], clamped[:], opened[:], MULT)
+                nc.sync.dma_start(
+                    out[b * P : (b + 1) * P, k * PIECE : (k + 1) * PIECE], product[:]
+                )

@@ -32,12 +32,12 @@ def tile_lookup_vg_cliprelu_out_kernel(tc, tab, offs, out):
         values = []
         gates = []
         for b in range(blocks):
-            value = held.tile([P, places], F32, name=f"value{b}")
-            nc.sync.dma_start(value[:], tab[0, b * P : (b + 1) * P, :])
-            values.append(value)
             gate = held.tile([P, places], F32, name=f"gate{b}")
             nc.sync.dma_start(gate[:], tab[1, b * P : (b + 1) * P, :])
             gates.append(gate)
+            value = held.tile([P, places], F32, name=f"value{b}")
+            nc.sync.dma_start(value[:], tab[0, b * P : (b + 1) * P, :])
+            values.append(value)
 
         for b in range(blocks):
             for k in range(pieces):

@@ -49,7 +49,9 @@ def tile_lookup_vg_cliprelu_out_kernel(tc, tab, offs, out):
                 opened = work.tile([P, PIECE], F32, name="opened")
                 nc.scalar.activation(opened[:], gates[b][:].indirect(piece), RELU)
                 product = work.tile([P, PIECE], F32, name="product")
-                nc.vector.tensor_tensor(product[:], clamped[:], opened[:], MULT)
+                last = b == blocks - 1 and k == pieces - 1
+                multiplier = nc.vector if last else nc.gpsimd
+                multiplier.tensor_tensor(product[:], clamped[:], opened[:], MULT)
                 nc.sync.dma_start(
                     out[b * P : (b + 1) * P, k * PIECE : (k + 1) * PIECE], product[:]
                 )

@@ -26,20 +26,26 @@ def tile_lookup_vg_cliprelu_out_kernel(tc, tab, offs, out):
         tc.tile_pool(name="held", bufs=1) as held,
         tc.tile_pool(name="work", bufs=blocks * pieces) as work,
     ):
+        zeros = held.tile([P, 1], F32, name="zeros")
+        nc.vector.memset(zeros[:], 0.0)
+        warm = held.tile([P, 1], F32, name="warm")
+        nc.scalar.activation(warm[:], zeros[:], RELU)
+
         offsets = held.tile([P, n // STRIPE], U16, name="offsets")
         nc.sync.dma_start(offsets[:], offs)
 
         values = []
         gates = []
         for b in range(blocks):
-            gate = held.tile([P, places], F32, name=f"gate{b}")
-            nc.sync.dma_start(gate[:], tab[1, b * P : (b + 1) * P, :])
-            gates.append(gate)
             value = held.tile([P, places], F32, name=f"value{b}")
             nc.sync.dma_start(value[:], tab[0, b * P : (b + 1) * P, :])
             values.append(value)
+            gate = held.tile([P, places], F32, name=f"gate{b}")
+            nc.sync.dma_start(gate[:], tab[1, b * P : (b + 1) * P, :])
+            gates.append(gate)
 
         for b in range(blocks):
+            looked_up = []
             for k in range(pieces):
                 piece = offsets[:, k * columns : (k + 1) * columns]
                 clamped = work.tile([P, PIECE], F32, name="clamped")
@@ -48,10 +54,18 @@ def tile_lookup_vg_cliprelu_out_kernel(tc, tab, offs, out):
                 )
                 opened = work.tile([P, PIECE], F32, name="opened")
                 nc.scalar.activation(opened[:], gates[b][:].indirect(piece), RELU)
-                product = work.tile([P, PIECE], F32, name="product")
-                last = b == blocks - 1 and k == pieces - 1
-                multiplier = nc.vector if last else nc.gpsimd
-                multiplier.tensor_tensor(product[:], clamped[:], opened[:], MULT)
-                nc.sync.dma_start(
-                    out[b * P : (b + 1) * P, k * PIECE : (k + 1) * PIECE], product[:]
-                )
+                looked_up.append((clamped, opened))
+
+            for k, (clamped, opened) in enumerate(looked_up):
+                ending = b == blocks - 1 and k >= pieces - 2
+                multiplier = nc.vector if ending else nc.gpsimd
+                parts = 2 if ending else 1
+                width = PIECE // parts
+                for h in range(parts):
+                    span = slice(h * width, (h + 1) * width)
+                    start = k * PIECE + h * width
+                    product = work.tile([P, width], F32, name=f"product{width}")
+                    multiplier.tensor_tensor(product[:], clamped[:, span], opened[:, span], MULT)
+                    nc.sync.dma_start(
+                        out[b * P : (b + 1) * P, start : start + width], product[:]
+                    )

import concourse.mybir as mybir

F32 = mybir.dt.float32
U16 = mybir.dt.uint16
MAX = mybir.AluOpType.max
MIN = mybir.AluOpType.min
MULT = mybir.AluOpType.mult
RELU = mybir.ActivationFunctionType.Relu

P = 128
PIECE = 512
STRIPE = 16

FLOPS = 4 * 256 * 2048


def tile_lookup_vg_cliprelu_out_kernel(tc, tab, offs, out):
    nc = tc.nc
    rows, places = tab.shape[1], tab.shape[2]
    n = out.shape[1]
    blocks = rows // P
    pieces = n // PIECE
    columns = PIECE // STRIPE

    with (
        tc.tile_pool(name="held", bufs=1) as held,
        tc.tile_pool(name="work", bufs=blocks * pieces) as work,
    ):
        zeros = held.tile([P, 1], F32, name="zeros")
        nc.vector.memset(zeros[:], 0.0)
        warm = held.tile([P, 1], F32, name="warm")
        nc.scalar.activation(warm[:], zeros[:], RELU)

        offsets = held.tile([P, n // STRIPE], U16, name="offsets")
        nc.sync.dma_start(offsets[:], offs)

        values = []
        gates = []
        for b in range(blocks):
            value = held.tile([P, places], F32, name=f"value{b}")
            nc.sync.dma_start(value[:], tab[0, b * P : (b + 1) * P, :])
            values.append(value)
            gate = held.tile([P, places], F32, name=f"gate{b}")
            nc.sync.dma_start(gate[:], tab[1, b * P : (b + 1) * P, :])
            gates.append(gate)

        for b in range(blocks):
            looked_up = []
            for k in range(pieces):
                piece = offsets[:, k * columns : (k + 1) * columns]
                clamped = work.tile([P, PIECE], F32, name="clamped")
                nc.vector.tensor_scalar(
                    clamped[:], values[b][:].indirect(piece), -1.25, 1.0, MAX, MIN
                )
                opened = work.tile([P, PIECE], F32, name="opened")
                nc.scalar.activation(opened[:], gates[b][:].indirect(piece), RELU)
                looked_up.append((clamped, opened))

            for k, (clamped, opened) in enumerate(looked_up):
                ending = b == blocks - 1 and k >= pieces - 2
                multiplier = nc.vector if ending else nc.gpsimd
                parts = 2 if ending else 1
                width = PIECE // parts
                for h in range(parts):
                    span = slice(h * width, (h + 1) * width)
                    start = k * PIECE + h * width
                    product = work.tile([P, width], F32, name=f"product{width}")
                    multiplier.tensor_tensor(product[:], clamped[:, span], opened[:, span], MULT)
                    nc.sync.dma_start(
                        out[b * P : (b + 1) * P, start : start + width], product[:]
                    )
